import numpy as np
import ml_dtypes


def mxq(x, axis, fmt="e4m3"):
    dtype, down = {"e4m3": (ml_dtypes.float8_e4m3fn, 7), "e5m2": (ml_dtypes.float8_e5m2, 14)}[fmt]
    v = np.moveaxis(np.asarray(x, np.float32).astype(ml_dtypes.bfloat16).astype(np.float64), axis, -1)
    blocks = v.reshape(v.shape[:-1] + (-1, 32))
    amax = np.abs(blocks).max(-1, keepdims=True)
    byte = np.maximum(np.where(amax > 0, np.frexp(amax)[1] - 1 + 127, 0) - down, 1)
    scale = np.exp2(byte - 127.0)
    codes = (blocks / scale).astype(np.float32).astype(dtype).astype(np.float64)
    return np.moveaxis((codes * scale).reshape(v.shape), -1, axis)


WIDE = False


def mx_kscale(k, group=512):
    if not WIDE:
        return np.ones(k)
    levels = np.array([10, -10, 5, -5, 0])
    if group != 512:
        return np.exp2(np.random.permutation(np.resize(levels, k // group))).repeat(group)
    if k % 512:
        return np.exp2(np.random.permutation(np.resize(levels, k // 32))).repeat(32)
    a = np.empty((k // 512, 16))
    for p in range(k // 512):
        a[p, :8] = np.random.permutation(np.resize(levels, 8))
        for g in range(8):
            far = levels[np.abs(levels - a[p, g]) >= 10]
            a[p, g + 8] = far[np.random.randint(len(far))]
    return np.exp2(a.ravel()).repeat(32)


def f64(x):
    return np.asarray(x).astype(np.float64)


G, D, M, N, L = 2, 256, 128, 512, 640


def setup_inputs():
    n = np.random.standard_normal
    s_d = mx_kscale(D, 0)
    return {
        "x": (n((G, D, L)) * s_d[:, None]).astype(np.float32),
        "w0": (n((G, D, M)) / np.sqrt(2 * D) / s_d[:, None]).astype(np.float32),
        "w1": (n((G, D, M)) / np.sqrt(2 * D) / s_d[:, None]).astype(np.float32),
        "se": (np.random.uniform(0.1, 1.0, (G, M, 1))).astype(np.float32),
        "r": (n((G, M, N))).astype(np.float32),
    }


def reference(x, w0, w1, se, r):
    w0q = mxq(f64(w0), 1, "e4m3")
    xq = mxq(f64(x), 1, "e4m3")
    w1q = mxq(f64(w1), 1, "e4m3")
    z = (w0q.transpose(0, 2, 1) @ xq[..., :512]) + (w1q.transpose(0, 2, 1) @ xq[..., 128 : 640])
    y = z * f64(se) + f64(r)
    return y

@@ -1,0 +1,123 @@
+from contextlib import ExitStack
+
+import concourse.mybir as mybir
+
+G, D, M, N, L = 2, 256, 128, 512, 640
+FLOPS = 2 * 2 * G * D * M * N
+
+F32 = mybir.dt.float32
+BF16 = mybir.dt.bfloat16
+U32 = mybir.dt.uint32
+U8 = mybir.dt.uint8
+FP8X4 = mybir.dt.float8_e4m3fn_x4
+ALU = mybir.AluOpType
+
+P = 128
+PACK = 4
+ROWS = D // PACK
+NT = 128
+RUN = 4
+X_FIRST = 512
+STORE = 256
+
+
+def interleave(copy, grouped, raw, src0, dst0, count):
+    copy(
+        out=grouped[:, dst0 : dst0 + count, :].rearrange("p (c i) t -> p c t i", i=RUN),
+        in_=raw[:, :, src0 : src0 + count].rearrange("p t (c i) -> p c t i", i=RUN),
+    )
+
+
+def tile_rows_conv_se_kernel(tc, x, w0, w1, se, r, out):
+    nc = tc.nc
+
+    def by_partition(t):
+        return t.rearrange("g (p j) c -> (g p) j c", j=PACK)
+
+    with ExitStack() as ctx:
+        sb = ctx.enter_context(tc.tile_pool(name="sb", bufs=1))
+        psum = ctx.enter_context(tc.psum_pool(name="psum", bufs=1))
+        ctx.enter_context(tc.manual_schedule())
+
+        xa_raw = sb.tile([P, PACK, X_FIRST], F32, name="xa_raw")
+        xc_raw = sb.tile([P, PACK, L - X_FIRST], F32, name="xc_raw")
+        w_raw = [sb.tile([P, PACK, M], F32, name="w_raw%d" % t) for t in range(2)]
+        r_sb = [sb.tile([P, N], F32, name="r_sb%d" % g) for g in range(G)]
+        se_sb = sb.tile([P, G, 8], F32, name="se_sb")
+
+        xp = by_partition(x)
+        nc.sync.dma_start(out=xa_raw[:], in_=xp[:, :, 0:X_FIRST])
+        with nc.allow_non_contiguous_dma(reason="one factor a partition"):
+            nc.scalar.dma_start(out=se_sb[:, :, 0:1], in_=se.rearrange("g m o -> m g o"))
+        nc.sync.dma_start(out=w_raw[0][:], in_=by_partition(w0))
+        nc.sync.dma_start(out=w_raw[1][:], in_=by_partition(w1))
+        nc.sync.dma_start(out=xc_raw[:], in_=xp[:, :, X_FIRST:L])
+        for g in range(G):
+            nc.sync.dma_start(out=r_sb[g][:], in_=r[g])
+
+        def operand(name, width):
+            grouped = sb.tile([P, width, PACK], BF16, name=name + "_bf", align_bytes=64)
+            codes = sb.tile([P, width], U32, name=name + "_codes", align_bytes=64)
+            scales = sb.tile([P, width], U8, name=name + "_scales", align_bytes=64)
+            return grouped, codes, scales
+
+        def quantize(op):
+            nc.vector.quantize_mx(
+                out=op[1][:].bitcast(FP8X4),
+                scales=op[2][:],
+                in_=op[0][:].rearrange("p w j -> p (w j)"),
+            )
+
+        x01 = operand("x01", 256)
+        x23 = operand("x23", 256)
+        x4 = operand("x4", 128)
+        wq = [operand("wq%d" % t, M) for t in range(2)]
+        x_piece = [(x01, 0), (x01, 128), (x23, 0), (x23, 128), (x4, 0)]
+
+        acc = [[psum.tile([M, NT], F32, name="acc%d_%d" % (g, c)) for c in range(N // NT)] for g in range(G)]
+
+        def tap(t, c):
+            op, c0 = x_piece[c + t]
+            for g in range(G):
+                rows = slice(g * ROWS, (g + 1) * ROWS)
+                nc.tensor.matmul_mx(
+                    out=acc[g][c][:],
+                    lhsT=wq[t][1][rows, :].bitcast(FP8X4),
+                    lhsT_scale=wq[t][2][rows, :],
+                    rhs=op[1][rows, c0 : c0 + NT].bitcast(FP8X4),
+                    rhs_scale=op[2][rows, c0 : c0 + NT],
+                    start=(t == 0),
+                    stop=(t == 1),
+                )
+
+        interleave(nc.vector.tensor_copy, x01[0], xa_raw, 0, 0, 256)
+        interleave(nc.scalar.copy, x23[0], xa_raw, 384, 128, 128)
+        interleave(nc.vector.tensor_copy, x23[0], xa_raw, 256, 0, 128)
+        interleave(nc.scalar.copy, wq[0][0], w_raw[0], 0, 0, M)
+        interleave(nc.scalar.copy, wq[1][0], w_raw[1], 0, 0, M)
+        quantize(x01)
+        quantize(wq[0])
+        quantize(x23)
+        for c in range(4):
+            tap(0, c)
+        quantize(wq[1])
+        for c in range(3):
+            tap(1, c)
+        interleave(nc.vector.tensor_copy, x4[0], xc_raw, 0, 0, 88)
+        interleave(nc.scalar.copy, x4[0], xc_raw, 88, 88, 40)
+        quantize(x4)
+        tap(1, 3)
+
+        for g in range(G):
+            for s0 in range(0, N, STORE):
+                y = sb.tile([P, STORE], F32, name="y%d_%d" % (g, s0))
+                for c0 in range(s0, s0 + STORE, NT):
+                    nc.vector.scalar_tensor_tensor(
+                        out=y[:, c0 - s0 : c0 - s0 + NT],
+                        in0=acc[g][c0 // NT][:],
+                        scalar=se_sb[:, g, 0:1],
+                        in1=r_sb[g][:, c0 : c0 + NT],
+                        op0=ALU.mult,
+                        op1=ALU.add,
+                    )
+                nc.sync.dma_start(out=out[g, :, s0 : s0 + STORE], in_=y[:])

@@ -17,8 +17,6 @@ PACK = 4
 ROWS = D // PACK
 NT = 128
 RUN = 4
-X_FIRST = 512
-STORE = 256
 
 
 def interleave(copy, grouped, raw, src0, dst0, count):
@@ -39,21 +37,23 @@ def tile_rows_conv_se_kernel(tc, x, w0, w1, se, r, out):
         psum = ctx.enter_context(tc.psum_pool(name="psum", bufs=1))
         ctx.enter_context(tc.manual_schedule())
 
-        xa_raw = sb.tile([P, PACK, X_FIRST], F32, name="xa_raw")
-        xc_raw = sb.tile([P, PACK, L - X_FIRST], F32, name="xc_raw")
         w_raw = [sb.tile([P, PACK, M], F32, name="w_raw%d" % t) for t in range(2)]
         r_sb = [sb.tile([P, N], F32, name="r_sb%d" % g) for g in range(G)]
-        se_sb = sb.tile([P, G, 8], F32, name="se_sb")
-
+        se_rows = sb.tile([P, P], F32, name="se_rows", align_bytes=64)
+        se_sb = sb.tile([P, P], F32, name="se_sb", align_bytes=64)
         xp = by_partition(x)
-        nc.sync.dma_start(out=xa_raw[:], in_=xp[:, :, 0:X_FIRST])
-        with nc.allow_non_contiguous_dma(reason="one factor a partition"):
-            nc.scalar.dma_start(out=se_sb[:, :, 0:1], in_=se.rearrange("g m o -> m g o"))
-        nc.sync.dma_start(out=w_raw[0][:], in_=by_partition(w0))
-        nc.sync.dma_start(out=w_raw[1][:], in_=by_partition(w1))
-        nc.sync.dma_start(out=xc_raw[:], in_=xp[:, :, X_FIRST:L])
-        for g in range(G):
-            nc.sync.dma_start(out=r_sb[g][:], in_=r[g])
+
+        def load_x(c0, c1, q=nc.sync):
+            raw = sb.tile([P, PACK, c1 - c0], F32, name="x_raw%d" % c0)
+            q.dma_start(out=raw[:], in_=xp[:, :, c0:c1])
+            return raw
+
+        def load_se(q):
+            nc.vector.memset(se_rows[:], 0.0)
+            q.dma_start(
+                out=se_rows[0:P:32, 0 : G * 32].rearrange("q (g i) -> q g i", g=G),
+                in_=se.rearrange("g (q i) o -> q g (i o)", i=32),
+            )
 
         def operand(name, width):
             grouped = sb.tile([P, width, PACK], BF16, name=name + "_bf", align_bytes=64)
@@ -68,17 +68,13 @@ def tile_rows_conv_se_kernel(tc, x, w0, w1, se, r, out):
                 in_=op[0][:].rearrange("p w j -> p (w j)"),
             )
 
-        x01 = operand("x01", 256)
-        x23 = operand("x23", 256)
-        x4 = operand("x4", 128)
         wq = [operand("wq%d" % t, M) for t in range(2)]
-        x_piece = [(x01, 0), (x01, 128), (x23, 0), (x23, 128), (x4, 0)]
-
         acc = [[psum.tile([M, NT], F32, name="acc%d_%d" % (g, c)) for c in range(N // NT)] for g in range(G)]
+        x_piece = []
 
-        def tap(t, c):
+        def tap(t, c, groups=(0, 1)):
             op, c0 = x_piece[c + t]
-            for g in range(G):
+            for g in groups:
                 rows = slice(g * ROWS, (g + 1) * ROWS)
                 nc.tensor.matmul_mx(
                     out=acc[g][c][:],
@@ -90,34 +86,75 @@ def tile_rows_conv_se_kernel(tc, x, w0, w1, se, r, out):
                     stop=(t == 1),
                 )
 
-        interleave(nc.vector.tensor_copy, x01[0], xa_raw, 0, 0, 256)
-        interleave(nc.scalar.copy, x23[0], xa_raw, 384, 128, 128)
-        interleave(nc.vector.tensor_copy, x23[0], xa_raw, 256, 0, 128)
-        interleave(nc.scalar.copy, wq[0][0], w_raw[0], 0, 0, M)
-        interleave(nc.scalar.copy, wq[1][0], w_raw[1], 0, 0, M)
-        quantize(x01)
-        quantize(wq[0])
-        quantize(x23)
-        for c in range(4):
-            tap(0, c)
-        quantize(wq[1])
-        for c in range(3):
-            tap(1, c)
-        interleave(nc.vector.tensor_copy, x4[0], xc_raw, 0, 0, 88)
-        interleave(nc.scalar.copy, x4[0], xc_raw, 88, 88, 40)
-        quantize(x4)
-        tap(1, 3)
+        y = [[sb.tile([P, 2 * NT], F32, name="y%d_%d" % (g, h)) for h in range(2)] for g in range(G)]
 
+        def finish(g, c):
+            nc.vector.scalar_tensor_tensor(
+                out=y[g][c // 2][:, (c % 2) * NT : (c % 2 + 1) * NT],
+                in0=acc[g][c][:],
+                scalar=se_sb[:, 32 * g : 32 * g + 1],
+                in1=r_sb[g][:, c * NT : (c + 1) * NT],
+                op0=ALU.mult,
+                op1=ALU.add,
+            )
+
+        def store(g, h, q=nc.sync):
+            q.dma_start(out=out[g, :, h * 2 * NT : (h + 1) * 2 * NT], in_=y[g][h][:])
+
+        vcopy = nc.vector.tensor_copy
+        scopy = nc.scalar.copy
+
+        xa = load_x(0, 512)
+        load_se(nc.sync)
+        nc.sync.dma_start(out=w_raw[0][:], in_=by_partition(w0))
+        nc.sync.dma_start(out=w_raw[1][:], in_=by_partition(w1))
+        xc = load_x(512, 640)
         for g in range(G):
-            for s0 in range(0, N, STORE):
-                y = sb.tile([P, STORE], F32, name="y%d_%d" % (g, s0))
-                for c0 in range(s0, s0 + STORE, NT):
-                    nc.vector.scalar_tensor_tensor(
-                        out=y[:, c0 - s0 : c0 - s0 + NT],
-                        in0=acc[g][c0 // NT][:],
-                        scalar=se_sb[:, g, 0:1],
-                        in1=r_sb[g][:, c0 : c0 + NT],
-                        op0=ALU.mult,
-                        op1=ALU.add,
-                    )
-                nc.sync.dma_start(out=out[g, :, s0 : s0 + STORE], in_=y[:])
+            nc.sync.dma_start(out=r_sb[g][:], in_=r[g])
+
+        x0 = operand("x0", 128)
+        x1 = operand("x1", 128)
+        x23 = operand("x23", 256)
+        x4 = operand("x4", 128)
+        x_piece.extend([(x0, 0), (x1, 0), (x23, 0), (x23, 128), (x4, 0)])
+
+        def shared(op, raw):
+            interleave(vcopy, op[0], raw, 0, 0, 88)
+            interleave(scopy, op[0], raw, 88, 88, 40)
+
+        interleave(vcopy, x0[0], xa, 0, 0, 128)
+        interleave(vcopy, x1[0], xa, 128, 0, 128)
+        interleave(scopy, x23[0], xa, 384, 128, 128)
+        quantize(x0)
+        shared(wq[0], w_raw[0])
+        quantize(x1)
+        quantize(wq[0])
+        interleave(scopy, x23[0], xa, 256, 0, 128)
+        shared(wq[1], w_raw[1])
+        quantize(x23)
+        quantize(wq[1])
+        nc.vector.transpose(out=se_sb[:], in_=se_rows[:])
+        shared(x4, xc)
+        quantize(x4)
+
+        tap(0, 0, (0,))
+        tap(0, 1, (0,))
+        tap(0, 0, (1,))
+        tap(0, 1, (1,))
+        tap(1, 0, (0,))
+        tap(1, 1, (0,))
+        tap(0, 2, (0,))
+        tap(1, 2, (0,))
+        tap(0, 3, (0,))
+        tap(1, 0, (1,))
+        tap(1, 3, (0,))
+        tap(1, 1, (1,))
+        tap(0, 2, (1,))
+        tap(1, 2, (1,))
+        tap(0, 3, (1,))
+        tap(1, 3, (1,))
+        for g in range(G):
+            for h in range(2):
+                finish(g, 2 * h)
+                finish(g, 2 * h + 1)
+                store(g, h)

@@ -104,55 +104,45 @@ def tile_rows_conv_se_kernel(tc, x, w0, w1, se, r, out):
         vcopy = nc.vector.tensor_copy
         scopy = nc.scalar.copy
 
-        xa = load_x(0, 512)
-        load_se(nc.sync)
         nc.sync.dma_start(out=w_raw[0][:], in_=by_partition(w0))
+        load_se(nc.sync)
+        xa = load_x(0, 384)
         nc.sync.dma_start(out=w_raw[1][:], in_=by_partition(w1))
-        xc = load_x(512, 640)
+        xb = load_x(384, L)
         for g in range(G):
             nc.sync.dma_start(out=r_sb[g][:], in_=r[g])
 
-        x0 = operand("x0", 128)
-        x1 = operand("x1", 128)
-        x23 = operand("x23", 256)
-        x4 = operand("x4", 128)
-        x_piece.extend([(x0, 0), (x1, 0), (x23, 0), (x23, 128), (x4, 0)])
+        xq = [operand("x%d" % i, NT) for i in range(5)]
+        x_piece.extend([(op, 0) for op in xq])
 
-        def shared(op, raw):
-            interleave(vcopy, op[0], raw, 0, 0, 88)
-            interleave(scopy, op[0], raw, 88, 88, 40)
+        def shared(op, raw, c0=0):
+            interleave(vcopy, op[0], raw, c0, 0, 88)
+            interleave(scopy, op[0], raw, c0 + 88, 88, 40)
 
-        interleave(vcopy, x0[0], xa, 0, 0, 128)
-        interleave(vcopy, x1[0], xa, 128, 0, 128)
-        interleave(scopy, x23[0], xa, 384, 128, 128)
-        quantize(x0)
-        shared(wq[0], w_raw[0])
-        quantize(x1)
-        quantize(wq[0])
-        interleave(scopy, x23[0], xa, 256, 0, 128)
-        shared(wq[1], w_raw[1])
-        quantize(x23)
-        quantize(wq[1])
+        interleave(vcopy, wq[0][0], w_raw[0], 0, 0, M)
         nc.vector.transpose(out=se_sb[:], in_=se_rows[:])
-        shared(x4, xc)
-        quantize(x4)
+        quantize(wq[0])
+        shared(xq[0], xa)
+        interleave(vcopy, xq[1][0], xa, NT, 0, NT)
+        interleave(scopy, xq[2][0], xa, 2 * NT, 0, NT)
+        quantize(xq[0])
+        quantize(xq[1])
+        shared(wq[1], w_raw[1])
+        quantize(xq[2])
+        quantize(wq[1])
+        shared(xq[3], xb)
+        shared(xq[4], xb, NT)
+        quantize(xq[3])
+        quantize(xq[4])
 
-        tap(0, 0, (0,))
-        tap(0, 1, (0,))
-        tap(0, 0, (1,))
-        tap(0, 1, (1,))
-        tap(1, 0, (0,))
-        tap(1, 1, (0,))
-        tap(0, 2, (0,))
-        tap(1, 2, (0,))
-        tap(0, 3, (0,))
-        tap(1, 0, (1,))
-        tap(1, 3, (0,))
-        tap(1, 1, (1,))
-        tap(0, 2, (1,))
-        tap(1, 2, (1,))
-        tap(0, 3, (1,))
-        tap(1, 3, (1,))
+        for c in range(3):
+            tap(0, c)
+        for c in range(2):
+            tap(1, c)
+        for g in range(G):
+            tap(1, 2, (g,))
+            tap(0, 3, (g,))
+            tap(1, 3, (g,))
         for g in range(G):
             for h in range(2):
                 finish(g, 2 * h)

from contextlib import ExitStack

import concourse.mybir as mybir

G, D, M, N, L = 2, 256, 128, 512, 640
FLOPS = 2 * 2 * G * D * M * N

F32 = mybir.dt.float32
BF16 = mybir.dt.bfloat16
U32 = mybir.dt.uint32
U8 = mybir.dt.uint8
FP8X4 = mybir.dt.float8_e4m3fn_x4
ALU = mybir.AluOpType

P = 128
PACK = 4
ROWS = D // PACK
NT = 128
RUN = 4


def interleave(copy, grouped, raw, src0, dst0, count):
    copy(
        out=grouped[:, dst0 : dst0 + count, :].rearrange("p (c i) t -> p c t i", i=RUN),
        in_=raw[:, :, src0 : src0 + count].rearrange("p t (c i) -> p c t i", i=RUN),
    )


def tile_rows_conv_se_kernel(tc, x, w0, w1, se, r, out):
    nc = tc.nc

    def by_partition(t):
        return t.rearrange("g (p j) c -> (g p) j c", j=PACK)

    with ExitStack() as ctx:
        sb = ctx.enter_context(tc.tile_pool(name="sb", bufs=1))
        psum = ctx.enter_context(tc.psum_pool(name="psum", bufs=1))
        ctx.enter_context(tc.manual_schedule())

        w_raw = [sb.tile([P, PACK, M], F32, name="w_raw%d" % t) for t in range(2)]
        r_sb = [sb.tile([P, N], F32, name="r_sb%d" % g) for g in range(G)]
        se_rows = sb.tile([P, P], F32, name="se_rows", align_bytes=64)
        se_sb = sb.tile([P, P], F32, name="se_sb", align_bytes=64)
        xp = by_partition(x)

        def load_x(c0, c1, q=nc.sync):
            raw = sb.tile([P, PACK, c1 - c0], F32, name="x_raw%d" % c0)
            q.dma_start(out=raw[:], in_=xp[:, :, c0:c1])
            return raw

        def load_se(q):
            nc.vector.memset(se_rows[:], 0.0)
            q.dma_start(
                out=se_rows[0:P:32, 0 : G * 32].rearrange("q (g i) -> q g i", g=G),
                in_=se.rearrange("g (q i) o -> q g (i o)", i=32),
            )

        def operand(name, width):
            grouped = sb.tile([P, width, PACK], BF16, name=name + "_bf", align_bytes=64)
            codes = sb.tile([P, width], U32, name=name + "_codes", align_bytes=64)
            scales = sb.tile([P, width], U8, name=name + "_scales", align_bytes=64)
            return grouped, codes, scales

        def quantize(op):
            nc.vector.quantize_mx(
                out=op[1][:].bitcast(FP8X4),
                scales=op[2][:],
                in_=op[0][:].rearrange("p w j -> p (w j)"),
            )

        wq = [operand("wq%d" % t, M) for t in range(2)]
        acc = [[psum.tile([M, NT], F32, name="acc%d_%d" % (g, c)) for c in range(N // NT)] for g in range(G)]
        x_piece = []

        def tap(t, c, groups=(0, 1)):
            op, c0 = x_piece[c + t]
            for g in groups:
                rows = slice(g * ROWS, (g + 1) * ROWS)
                nc.tensor.matmul_mx(
                    out=acc[g][c][:],
                    lhsT=wq[t][1][rows, :].bitcast(FP8X4),
                    lhsT_scale=wq[t][2][rows, :],
                    rhs=op[1][rows, c0 : c0 + NT].bitcast(FP8X4),
                    rhs_scale=op[2][rows, c0 : c0 + NT],
                    start=(t == 0),
                    stop=(t == 1),
                )

        y = [[sb.tile([P, 2 * NT], F32, name="y%d_%d" % (g, h)) for h in range(2)] for g in range(G)]

        def finish(g, c):
            nc.vector.scalar_tensor_tensor(
                out=y[g][c // 2][:, (c % 2) * NT : (c % 2 + 1) * NT],
                in0=acc[g][c][:],
                scalar=se_sb[:, 32 * g : 32 * g + 1],
                in1=r_sb[g][:, c * NT : (c + 1) * NT],
                op0=ALU.mult,
                op1=ALU.add,
            )

        def store(g, h, q=nc.sync):
            q.dma_start(out=out[g, :, h * 2 * NT : (h + 1) * 2 * NT], in_=y[g][h][:])

        vcopy = nc.vector.tensor_copy
        scopy = nc.scalar.copy

        nc.sync.dma_start(out=w_raw[0][:], in_=by_partition(w0))
        load_se(nc.sync)
        xa = load_x(0, 384)
        nc.sync.dma_start(out=w_raw[1][:], in_=by_partition(w1))
        xb = load_x(384, L)
        for g in range(G):
            nc.sync.dma_start(out=r_sb[g][:], in_=r[g])

        xq = [operand("x%d" % i, NT) for i in range(5)]
        x_piece.extend([(op, 0) for op in xq])

        def shared(op, raw, c0=0):
            interleave(vcopy, op[0], raw, c0, 0, 88)
            interleave(scopy, op[0], raw, c0 + 88, 88, 40)

        interleave(vcopy, wq[0][0], w_raw[0], 0, 0, M)
        nc.vector.transpose(out=se_sb[:], in_=se_rows[:])
        quantize(wq[0])
        shared(xq[0], xa)
        interleave(vcopy, xq[1][0], xa, NT, 0, NT)
        interleave(scopy, xq[2][0], xa, 2 * NT, 0, NT)
        quantize(xq[0])
        quantize(xq[1])
        shared(wq[1], w_raw[1])
        quantize(xq[2])
        quantize(wq[1])
        shared(xq[3], xb)
        shared(xq[4], xb, NT)
        quantize(xq[3])
        quantize(xq[4])

        for c in range(3):
            tap(0, c)
        for c in range(2):
            tap(1, c)
        for g in range(G):
            tap(1, 2, (g,))
            tap(0, 3, (g,))
            tap(1, 3, (g,))
        for g in range(G):
            for h in range(2):
                finish(g, 2 * h)
                finish(g, 2 * h + 1)
                store(g, h)
